import numpy as np
import ml_dtypes

BF16 = ml_dtypes.bfloat16


def bf(x):
    return np.asarray(x, np.float32).astype(BF16)


def f32(x):
    return np.asarray(x, np.float32)


def f64(x):
    return np.asarray(x).astype(np.float64)


def striped(idx):
    return np.tile(idx.reshape(-1, 16).T, (8, 1))


def rows(idx, k):
    return np.tile(idx, (k, 1))


def look(tab, idx):
    return np.take_along_axis(f64(tab), rows(idx, len(tab)), axis=1)


K, S, V, N = 256, 2048, 1024, 1024


def setup_inputs():
    return {"tab": f32(np.random.standard_normal((2, K, S))), "y": f32(1.0 * np.random.standard_normal((K, V))), "offs": striped(np.random.permutation(S)[:N])}


def reference(tab, y, offs):
    idx = offs[:16].T.reshape(-1)
    x = np.maximum(look(tab[0], idx), f64(y)) * np.tanh(look(tab[1], idx))
    return x

@@ -1,0 +1,38 @@
+import concourse.mybir as mybir
+
+F32, U16 = mybir.dt.float32, mybir.dt.uint16
+MAX, MULT = mybir.AluOpType.max, mybir.AluOpType.mult
+TANH = mybir.ActivationFunctionType.Tanh
+
+P = 128
+ROWS, PLACES, N = 256, 2048, 1024
+
+FLOPS = 3 * ROWS * N
+
+
+def tile_lookup_maxgate_out_kernel(tc, tab, y, offs, out):
+    nc = tc.nc
+    blocks = range(ROWS // P)
+    with tc.tile_pool(name="held", bufs=1) as held:
+        offsets = held.tile([P, N // 16], U16, name="offsets")
+        nc.sync.dma_start(offsets[:], offs)
+
+        floors, gates, stream = [], [], []
+        for b in blocks:
+            rows = slice(b * P, (b + 1) * P)
+            floors.append(held.tile([P, PLACES], F32, name=f"floors{b}"))
+            gates.append(held.tile([P, PLACES], F32, name=f"gates{b}"))
+            stream.append(held.tile([P, N], F32, name=f"stream{b}"))
+            nc.sync.dma_start(floors[b][:], tab[0, rows, :])
+            nc.sync.dma_start(stream[b][:], y[rows, :])
+            nc.sync.dma_start(gates[b][:], tab[1, rows, :])
+
+        for b in blocks:
+            rows = slice(b * P, (b + 1) * P)
+            floored = held.tile([P, N], F32, name=f"floored{b}")
+            gate = held.tile([P, N], F32, name=f"gate{b}")
+            product = held.tile([P, N], F32, name=f"product{b}")
+            nc.vector.tensor_tensor(floored[:], floors[b][:].indirect(offsets[:]), stream[b][:], MAX)
+            nc.scalar.activation(gate[:], gates[b][:].indirect(offsets[:]), TANH)
+            nc.vector.tensor_tensor(product[:], floored[:], gate[:], MULT)
+            nc.sync.dma_start(out[rows, :], product[:])

@@ -6,33 +6,36 @@ TANH = mybir.ActivationFunctionType.Tanh
 
 P = 128
 ROWS, PLACES, N = 256, 2048, 1024
-
-FLOPS = 3 * ROWS * N
+PIECE = N // 2
 
 
 def tile_lookup_maxgate_out_kernel(tc, tab, y, offs, out):
     nc = tc.nc
-    blocks = range(ROWS // P)
+    blocks = [slice(b * P, (b + 1) * P) for b in range(ROWS // P)]
+    pieces = [slice(j, j + PIECE) for j in range(0, N, PIECE)]
     with tc.tile_pool(name="held", bufs=1) as held:
         offsets = held.tile([P, N // 16], U16, name="offsets")
         nc.sync.dma_start(offsets[:], offs)
 
         floors, gates, stream = [], [], []
-        for b in blocks:
-            rows = slice(b * P, (b + 1) * P)
+        for b, rows in enumerate(blocks):
             floors.append(held.tile([P, PLACES], F32, name=f"floors{b}"))
             gates.append(held.tile([P, PLACES], F32, name=f"gates{b}"))
-            stream.append(held.tile([P, N], F32, name=f"stream{b}"))
+            stream.append([held.tile([P, PIECE], F32, name=f"stream{b}_{i}") for i in range(len(pieces))])
             nc.sync.dma_start(floors[b][:], tab[0, rows, :])
-            nc.sync.dma_start(stream[b][:], y[rows, :])
+            nc.sync.dma_start(stream[b][0][:], y[rows, pieces[0]])
             nc.sync.dma_start(gates[b][:], tab[1, rows, :])
+            nc.sync.dma_start(stream[b][1][:], y[rows, pieces[1]])
 
-        for b in blocks:
-            rows = slice(b * P, (b + 1) * P)
-            floored = held.tile([P, N], F32, name=f"floored{b}")
-            gate = held.tile([P, N], F32, name=f"gate{b}")
-            product = held.tile([P, N], F32, name=f"product{b}")
-            nc.vector.tensor_tensor(floored[:], floors[b][:].indirect(offsets[:]), stream[b][:], MAX)
-            nc.scalar.activation(gate[:], gates[b][:].indirect(offsets[:]), TANH)
-            nc.vector.tensor_tensor(product[:], floored[:], gate[:], MULT)
-            nc.sync.dma_start(out[rows, :], product[:])
+        for b, rows in enumerate(blocks):
+            floored, gate = [], []
+            for i, piece in enumerate(pieces):
+                entries = offsets[:, piece.start // 16 : piece.stop // 16]
+                floored.append(held.tile([P, PIECE], F32, name=f"floored{b}_{i}"))
+                gate.append(held.tile([P, PIECE], F32, name=f"gate{b}_{i}"))
+                nc.vector.tensor_tensor(floored[i][:], floors[b][:].indirect(entries), stream[b][i][:], MAX)
+                nc.scalar.activation(gate[i][:], gates[b][:].indirect(entries), TANH)
+            for i, piece in enumerate(pieces):
+                product = held.tile([P, PIECE], F32, name=f"product{b}_{i}")
+                nc.vector.tensor_tensor(product[:], floored[i][:], gate[i][:], MULT)
+                nc.sync.dma_start(out[rows, piece], product[:])

import concourse.mybir as mybir

F32, U16 = mybir.dt.float32, mybir.dt.uint16
MAX, MULT = mybir.AluOpType.max, mybir.AluOpType.mult
TANH = mybir.ActivationFunctionType.Tanh

P = 128
ROWS, PLACES, N = 256, 2048, 1024
PIECE = N // 2


def tile_lookup_maxgate_out_kernel(tc, tab, y, offs, out):
    nc = tc.nc
    blocks = [slice(b * P, (b + 1) * P) for b in range(ROWS // P)]
    pieces = [slice(j, j + PIECE) for j in range(0, N, PIECE)]
    with tc.tile_pool(name="held", bufs=1) as held:
        offsets = held.tile([P, N // 16], U16, name="offsets")
        nc.sync.dma_start(offsets[:], offs)

        floors, gates, stream = [], [], []
        for b, rows in enumerate(blocks):
            floors.append(held.tile([P, PLACES], F32, name=f"floors{b}"))
            gates.append(held.tile([P, PLACES], F32, name=f"gates{b}"))
            stream.append([held.tile([P, PIECE], F32, name=f"stream{b}_{i}") for i in range(len(pieces))])
            nc.sync.dma_start(floors[b][:], tab[0, rows, :])
            nc.sync.dma_start(stream[b][0][:], y[rows, pieces[0]])
            nc.sync.dma_start(gates[b][:], tab[1, rows, :])
            nc.sync.dma_start(stream[b][1][:], y[rows, pieces[1]])

        for b, rows in enumerate(blocks):
            floored, gate = [], []
            for i, piece in enumerate(pieces):
                entries = offsets[:, piece.start // 16 : piece.stop // 16]
                floored.append(held.tile([P, PIECE], F32, name=f"floored{b}_{i}"))
                gate.append(held.tile([P, PIECE], F32, name=f"gate{b}_{i}"))
                nc.vector.tensor_tensor(floored[i][:], floors[b][:].indirect(entries), stream[b][i][:], MAX)
                nc.scalar.activation(gate[i][:], gates[b][:].indirect(entries), TANH)
            for i, piece in enumerate(pieces):
                product = held.tile([P, PIECE], F32, name=f"product{b}_{i}")
                nc.vector.tensor_tensor(product[:], floored[i][:], gate[i][:], MULT)
                nc.sync.dma_start(out[rows, piece], product[:])
